import numpy as np
import ml_dtypes


def mxq(x, axis, fmt="e4m3"):
    dtype, down = {"e4m3": (ml_dtypes.float8_e4m3fn, 7), "e5m2": (ml_dtypes.float8_e5m2, 14)}[fmt]
    v = np.moveaxis(np.asarray(x, np.float32).astype(ml_dtypes.bfloat16).astype(np.float64), axis, -1)
    blocks = v.reshape(v.shape[:-1] + (-1, 32))
    amax = np.abs(blocks).max(-1, keepdims=True)
    byte = np.maximum(np.where(amax > 0, np.frexp(amax)[1] - 1 + 127, 0) - down, 1)
    scale = np.exp2(byte - 127.0)
    codes = (blocks / scale).astype(np.float32).astype(dtype).astype(np.float64)
    return np.moveaxis((codes * scale).reshape(v.shape), -1, axis)


WIDE = False


def mx_kscale(k, group=512):
    if not WIDE:
        return np.ones(k)
    levels = np.array([18, -18])
    if group != 512:
        return np.exp2(np.random.permutation(np.resize(levels, k // group))).repeat(group)
    if k % 512:
        return np.exp2(np.random.permutation(np.resize(levels, k // 32))).repeat(32)
    a = np.empty((k // 512, 16))
    for p in range(k // 512):
        a[p, :8] = np.random.permutation(np.resize(levels, 8))
        for g in range(8):
            far = levels[np.abs(levels - a[p, g]) >= 10]
            a[p, g + 8] = far[np.random.randint(len(far))]
    return np.exp2(a.ravel()).repeat(32)


def f64(x):
    return np.asarray(x).astype(np.float64)


G, D, J, K, L = 8, 128, 128, 128, 128


def setup_inputs():
    n = np.random.standard_normal
    s_d = mx_kscale(D, 0)
    s_j = mx_kscale(J, 0)
    return {
        "x": (n((G, D, J)) * s_d[:, None] * s_j).astype(np.float32),
        "a": (n((D, K)) / np.sqrt(D) / s_d[:, None]).astype(np.float32),
        "b": (n((J, L)) / np.sqrt(J) / s_j[:, None]).astype(np.float32),
        "th": (np.random.uniform(0.1, 0.6, (K, 1))).astype(np.float32),
    }


def reference(x, a, b, th):
    xq = mxq(f64(x), 1, "e4m3")
    aq = mxq(f64(a), 0, "e4m3")
    z = xq.transpose(0, 2, 1) @ aq
    zq = mxq(z, 1, "e4m3")
    bq = mxq(f64(b), 0, "e4m3")
    w = zq.transpose(0, 2, 1) @ bq
    y = np.maximum(w - f64(th), 0.0) - np.maximum(0.0 - w - f64(th), 0.0)
    return y

@@ -1,0 +1,151 @@
+from contextlib import ExitStack
+
+import concourse.mybir as mybir
+
+G, D, J, K, L = 8, 128, 128, 128, 128
+FLOPS = 2 * G * D * J * K + 2 * G * J * K * L
+
+F32 = mybir.dt.float32
+BF16 = mybir.dt.bfloat16
+U32 = mybir.dt.uint32
+U8 = mybir.dt.uint8
+I32 = mybir.dt.int32
+FP8X4 = mybir.dt.float8_e4m3fn_x4
+ALU = mybir.AluOpType
+ACT = mybir.ActivationFunctionType
+
+P = 128
+R = 32
+T = 4
+PAD = 64
+A_SCALAR = 18
+
+
+def tile_rows_kron_soft_kernel(tc, x, a, b, th, out):
+    nc = tc.nc
+    with ExitStack() as ctx:
+        sb = ctx.enter_context(tc.tile_pool(name="sb", bufs=1))
+        ps = ctx.enter_context(tc.psum_pool(name="ps", bufs=1))
+        ctx.enter_context(tc.manual_schedule())
+
+        x_raw = [sb.tile([P, T * J], F32, name="x_raw%d" % h) for h in range(2)]
+        a_raw = sb.tile([P, T * K], F32)
+        b_raw = sb.tile([P, T * L], F32)
+        th_pos = sb.tile([P, 1], F32)
+        th_neg = sb.tile([P, 1], F32)
+        x_bf = sb.tile([P, 2 * T * J], BF16, align_bytes=64)
+        a_bf = sb.tile([P, T * K], BF16, align_bytes=64)
+        b_bf = sb.tile([P, T * L], BF16, align_bytes=64)
+        x_codes = sb.tile([P, 2 * J + 2 * PAD], U32, align_bytes=64)
+        x_scales = sb.tile([P, 2 * J + 2 * PAD], U8, align_bytes=64)
+        a_codes = sb.tile([P, K], U32, align_bytes=64)
+        a_scales = sb.tile([P, K], U8, align_bytes=64)
+        b_codes = sb.tile([P, L], U32, align_bytes=64)
+        b_scales = sb.tile([P, L], U8, align_bytes=64)
+        z_bf = [sb.tile([P, T * K], BF16, align_bytes=64, name="z_bf%d" % m) for m in range(2)]
+        z_codes = [sb.tile([P, K], U32, align_bytes=64, name="z_codes%d" % m) for m in range(2)]
+        z_scales = [sb.tile([P, K], U8, align_bytes=64, name="z_scales%d" % m) for m in range(2)]
+        z_ps = [ps.tile([P, T * K], F32, name="z_ps%d" % r) for r in range(4)]
+        w_ps = [ps.tile([P, L], F32, name="w_ps%d" % r) for r in range(4)]
+
+        nc.gpsimd.dma_start(out=th_pos[:], in_=th)
+        for h in range(2):
+            nc.sync.dma_start(
+                out=x_raw[h][:], in_=x[4 * h : 4 * h + 4].rearrange("g (q s) j -> (g q) (s j)", s=T)
+            )
+        for src, dst in ((a, a_raw), (b, b_raw)):
+            for r in (0, 2, 1, 3):
+                nc.sync.dma_start(out=dst[R * r : R * r + R, :], in_=src.rearrange("(q s) c -> q (s c)", s=T))
+
+        for lo in (0, PAD + 2 * J):
+            nc.gpsimd.memset(x_codes[:, lo : lo + PAD].bitcast(I32), 0)
+            nc.gpsimd.memset(x_scales[:, lo : lo + PAD].bitcast(I32), 0)
+        nc.gpsimd.tensor_scalar(th_neg[:], th_pos[:], -1.0, 0.0, op0=ALU.mult, op1=ALU.add)
+
+        def x_views(h):
+            dst = x_bf[:].rearrange("p (t h u s) -> p h u s t", t=T, h=2, s=T)[:, h]
+            src = x_raw[h][:].rearrange("p (s u t) -> p u s t", s=T, t=T)
+            return dst, src
+
+        def factor_views(bf, raw):
+            dst = bf[:].rearrange("p (c i s) -> p c s i", i=4, s=T)
+            src = raw[:].rearrange("p (s c i) -> p c s i", s=T, i=4)
+            return dst, src
+
+        dst, src = x_views(0)
+        nc.scalar.copy(out=dst, in_=src)
+        dst, src = x_views(1)
+        nc.vector.tensor_copy(out=dst, in_=src)
+        nc.vector.quantize_mx(
+            out=x_codes[:, PAD : PAD + 2 * J].bitcast(FP8X4), scales=x_scales[:, PAD : PAD + 2 * J], in_=x_bf[:]
+        )
+        dst, src = factor_views(a_bf, a_raw)
+        nc.scalar.copy(out=dst[:, :A_SCALAR], in_=src[:, :A_SCALAR])
+        nc.vector.tensor_copy(out=dst[:, A_SCALAR:], in_=src[:, A_SCALAR:])
+        nc.vector.quantize_mx(out=a_codes[:].bitcast(FP8X4), scales=a_scales[:], in_=a_bf[:])
+        dst, src = factor_views(b_bf, b_raw)
+        nc.scalar.copy(out=dst, in_=src)
+
+        for t in range(T):
+            for r in (0, 2, 1, 3):
+                rows = slice(R * r, R * r + R)
+                lo = PAD + 2 * R * (t - r // 2)
+                nc.tensor.matmul_mx(
+                    out=z_ps[r][:, K * t : K * t + K],
+                    lhsT=x_codes[rows, lo : lo + P].bitcast(FP8X4),
+                    lhsT_scale=x_scales[rows, lo : lo + P],
+                    rhs=a_codes[rows, :].bitcast(FP8X4),
+                    rhs_scale=a_scales[rows, :],
+                    start=True,
+                    stop=True,
+                )
+        nc.vector.quantize_mx(out=b_codes[:].bitcast(FP8X4), scales=b_scales[:], in_=b_bf[:])
+
+        def z_views(r):
+            half = slice(2 * R * (r // 2), 2 * R * (r // 2) + 2 * R)
+            dst = z_bf[r % 2][half, :].rearrange("p (k t) -> p k t", t=T)
+            src = z_ps[r][half, :].rearrange("p (t k) -> p k t", t=T)
+            return dst, src
+
+        banks = [w_ps, z_ps]
+        for m in range(2):
+            dst, src = z_views(m)
+            nc.scalar.copy(out=dst, in_=src)
+            dst, src = z_views(2 + m)
+            nc.vector.tensor_copy(out=dst, in_=src)
+            nc.vector.quantize_mx(out=z_codes[m][:].bitcast(FP8X4), scales=z_scales[m][:], in_=z_bf[m][:])
+            for r in range(4):
+                rows = slice(R * r, R * r + R)
+                nc.tensor.matmul_mx(
+                    out=banks[m][r][:, :L],
+                    lhsT=z_codes[m][rows, :].bitcast(FP8X4),
+                    lhsT_scale=z_scales[m][rows, :],
+                    rhs=b_codes[rows, :].bitcast(FP8X4),
+                    rhs_scale=b_scales[rows, :],
+                    start=True,
+                    stop=True,
+                )
+
+        for m in range(2):
+            y_s = sb.tile([P, 2, L], F32, name="y_s%d" % m)
+            y_v = sb.tile([P, 2, L], F32, name="y_v%d" % m)
+            up = [sb.tile([P, L], F32, name="up%d_%d" % (m, i)) for i in range(4)]
+            down = [sb.tile([P, L], F32, name="down%d_%d" % (m, i)) for i in range(2)]
+            for i in range(2):
+                w = banks[m][2 * i][:, :L]
+                nc.scalar.activation(out=up[i][:], in_=w, func=ACT.Relu, bias=th_neg[:], scale=1.0)
+                nc.scalar.activation(out=down[i][:], in_=w, func=ACT.Relu, bias=th_neg[:], scale=-1.0)
+                nc.gpsimd.tensor_tensor(out=y_s[:, i, :], in0=up[i][:], in1=down[i][:], op=ALU.subtract)
+            for i in range(2):
+                nc.vector.tensor_scalar(up[2 + i][:], banks[m][2 * i + 1][:, :L], th_pos[:], None, op0=ALU.max)
+            for i in range(2):
+                nc.vector.scalar_tensor_tensor(
+                    out=y_v[:, i, :],
+                    in0=banks[m][2 * i + 1][:, :L],
+                    scalar=th_neg[:],
+                    in1=up[2 + i][:],
+                    op0=ALU.min,
+                    op1=ALU.add,
+                )
+            nc.sync.dma_start(out=out[4 + m : 8 : 2].rearrange("g k l -> k g l"), in_=y_v[:])
+            nc.sync.dma_start(out=out[m:4:2].rearrange("g k l -> k g l"), in_=y_s[:])

@@ -9,7 +9,6 @@ F32 = mybir.dt.float32
 BF16 = mybir.dt.bfloat16
 U32 = mybir.dt.uint32
 U8 = mybir.dt.uint8
-I32 = mybir.dt.int32
 FP8X4 = mybir.dt.float8_e4m3fn_x4
 ALU = mybir.AluOpType
 ACT = mybir.ActivationFunctionType
@@ -17,8 +16,8 @@ ACT = mybir.ActivationFunctionType
 P = 128
 R = 32
 T = 4
-PAD = 64
-A_SCALAR = 18
+TOP = 3 * R
+LAST_SCALAR = 10
 
 
 def tile_rows_kron_soft_kernel(tc, x, a, b, th, out):
@@ -28,16 +27,16 @@ def tile_rows_kron_soft_kernel(tc, x, a, b, th, out):
         ps = ctx.enter_context(tc.psum_pool(name="ps", bufs=1))
         ctx.enter_context(tc.manual_schedule())
 
-        x_raw = [sb.tile([P, T * J], F32, name="x_raw%d" % h) for h in range(2)]
+        x_raw = [sb.tile([P, T * J], F32, name="x_raw%d" % i) for i in range(4)]
         a_raw = sb.tile([P, T * K], F32)
         b_raw = sb.tile([P, T * L], F32)
         th_pos = sb.tile([P, 1], F32)
         th_neg = sb.tile([P, 1], F32)
-        x_bf = sb.tile([P, 2 * T * J], BF16, align_bytes=64)
+        x_bf = sb.tile([P, T * T * J], BF16, align_bytes=64)
         a_bf = sb.tile([P, T * K], BF16, align_bytes=64)
         b_bf = sb.tile([P, T * L], BF16, align_bytes=64)
-        x_codes = sb.tile([P, 2 * J + 2 * PAD], U32, align_bytes=64)
-        x_scales = sb.tile([P, 2 * J + 2 * PAD], U8, align_bytes=64)
+        x_codes = [sb.tile([P, J], U32, align_bytes=64, name="x_codes%d" % t) for t in range(T)]
+        x_scales = [sb.tile([P, J], U8, align_bytes=64, name="x_scales%d" % t) for t in range(T)]
         a_codes = sb.tile([P, K], U32, align_bytes=64)
         a_scales = sb.tile([P, K], U8, align_bytes=64)
         b_codes = sb.tile([P, L], U32, align_bytes=64)
@@ -45,55 +44,68 @@ def tile_rows_kron_soft_kernel(tc, x, a, b, th, out):
         z_bf = [sb.tile([P, T * K], BF16, align_bytes=64, name="z_bf%d" % m) for m in range(2)]
         z_codes = [sb.tile([P, K], U32, align_bytes=64, name="z_codes%d" % m) for m in range(2)]
         z_scales = [sb.tile([P, K], U8, align_bytes=64, name="z_scales%d" % m) for m in range(2)]
-        z_ps = [ps.tile([P, T * K], F32, name="z_ps%d" % r) for r in range(4)]
-        w_ps = [ps.tile([P, L], F32, name="w_ps%d" % r) for r in range(4)]
+        z_ps = [ps.tile([P, T * K], F32, name="z_ps%d" % m) for m in range(2)]
+        w_ps = {}
+        for m in range(2):
+            for r in range(4):
+                if m == 1 and r in (1, 2):
+                    w_ps[r, m] = z_ps[r - 1]
+                else:
+                    w_ps[r, m] = ps.tile([P, L], F32, name="w_ps%d_%d" % (r, m))
 
-        nc.gpsimd.dma_start(out=th_pos[:], in_=th)
-        for h in range(2):
+        nc.scalar.dma_start(out=th_pos[:], in_=th)
+        for r in (1, 2):
+            nc.sync.dma_start(out=a_raw[R * r : R * r + R, :], in_=a.rearrange("(q s) c -> q (s c)", s=T))
+        for i in range(4):
             nc.sync.dma_start(
-                out=x_raw[h][:], in_=x[4 * h : 4 * h + 4].rearrange("g (q s) j -> (g q) (s j)", s=T)
+                out=x_raw[i][R:TOP, :], in_=x[2 * i : 2 * i + 2].rearrange("g (q s) j -> (g q) (s j)", s=T)
             )
-        for src, dst in ((a, a_raw), (b, b_raw)):
-            for r in (0, 2, 1, 3):
-                nc.sync.dma_start(out=dst[R * r : R * r + R, :], in_=src.rearrange("(q s) c -> q (s c)", s=T))
+        for r in (0, 2, 1, 3):
+            nc.sync.dma_start(out=b_raw[R * r : R * r + R, :], in_=b.rearrange("(q s) c -> q (s c)", s=T))
 
-        for lo in (0, PAD + 2 * J):
-            nc.gpsimd.memset(x_codes[:, lo : lo + PAD].bitcast(I32), 0)
-            nc.gpsimd.memset(x_scales[:, lo : lo + PAD].bitcast(I32), 0)
-        nc.gpsimd.tensor_scalar(th_neg[:], th_pos[:], -1.0, 0.0, op0=ALU.mult, op1=ALU.add)
+        nc.scalar.mul(th_neg[:], th_pos[:], -1.0)
+        nc.vector.memset(a_raw[:R, :], 0.0)
+        for i in range(2):
+            nc.vector.memset(x_raw[i][:R, :], 0.0)
+            nc.gpsimd.memset(x_raw[2 + i][:R, :], 0.0)
 
-        def x_views(h):
-            dst = x_bf[:].rearrange("p (t h u s) -> p h u s t", t=T, h=2, s=T)[:, h]
-            src = x_raw[h][:].rearrange("p (s u t) -> p u s t", s=T, t=T)
+        def x_views(i):
+            dst = x_bf[:TOP, :].rearrange("p (t i u s) -> p i u s t", t=T, i=4, s=T)[:, i]
+            src = x_raw[i][:TOP, :].rearrange("p (s u t) -> p u s t", s=T, t=T)
             return dst, src
 
         def factor_views(bf, raw):
-            dst = bf[:].rearrange("p (c i s) -> p c s i", i=4, s=T)
-            src = raw[:].rearrange("p (s c i) -> p c s i", s=T, i=4)
+            dst = bf.rearrange("p (c i s) -> p c s i", i=4, s=T)
+            src = raw.rearrange("p (s c i) -> p c s i", s=T, i=4)
             return dst, src
 
-        dst, src = x_views(0)
+        dst, src = factor_views(a_bf[:TOP, :], a_raw[:TOP, :])
         nc.scalar.copy(out=dst, in_=src)
-        dst, src = x_views(1)
+        dst, src = x_views(0)
         nc.vector.tensor_copy(out=dst, in_=src)
-        nc.vector.quantize_mx(
-            out=x_codes[:, PAD : PAD + 2 * J].bitcast(FP8X4), scales=x_scales[:, PAD : PAD + 2 * J], in_=x_bf[:]
-        )
-        dst, src = factor_views(a_bf, a_raw)
-        nc.scalar.copy(out=dst[:, :A_SCALAR], in_=src[:, :A_SCALAR])
-        nc.vector.tensor_copy(out=dst[:, A_SCALAR:], in_=src[:, A_SCALAR:])
-        nc.vector.quantize_mx(out=a_codes[:].bitcast(FP8X4), scales=a_scales[:], in_=a_bf[:])
-        dst, src = factor_views(b_bf, b_raw)
+        dst, src = x_views(1)
+        nc.scalar.copy(out=dst, in_=src)
+        dst, src = x_views(2)
+        nc.vector.tensor_copy(out=dst, in_=src)
+        dst, src = x_views(3)
+        nc.scalar.copy(out=dst[:, :LAST_SCALAR], in_=src[:, :LAST_SCALAR])
+        nc.vector.tensor_copy(out=dst[:, LAST_SCALAR:], in_=src[:, LAST_SCALAR:])
+        nc.vector.quantize_mx(out=a_codes[:TOP, :].bitcast(FP8X4), scales=a_scales[:TOP, :], in_=a_bf[:TOP, :])
+        dst, src = factor_views(b_bf[:], b_raw[:])
         nc.scalar.copy(out=dst, in_=src)
 
         for t in range(T):
-            for r in (0, 2, 1, 3):
-                rows = slice(R * r, R * r + R)
-                lo = PAD + 2 * R * (t - r // 2)
+            nc.vector.quantize_mx(
+                out=x_codes[t][:TOP, :].bitcast(FP8X4),
+                scales=x_scales[t][:TOP, :],
+                in_=x_bf[:TOP, T * J * t : T * J * (t + 1)],
+            )
+            for m in range(2):
+                rows = slice(R * (1 + m), R * (2 + m))
                 nc.tensor.matmul_mx(
-                    out=z_ps[r][:, K * t : K * t + K],
-                    lhsT=x_codes[rows, lo : lo + P].bitcast(FP8X4),
-                    lhsT_scale=x_scales[rows, lo : lo + P],
+                    out=z_ps[m][:, K * t : K * t + K],
+                    lhsT=x_codes[t][rows, :].bitcast(FP8X4),
+                    lhsT_scale=x_scales[t][rows, :],
                     rhs=a_codes[rows, :].bitcast(FP8X4),
                     rhs_scale=a_scales[rows, :],
                     start=True,
@@ -101,23 +113,21 @@ def tile_rows_kron_soft_kernel(tc, x, a, b, th, out):
                 )
         nc.vector.quantize_mx(out=b_codes[:].bitcast(FP8X4), scales=b_scales[:], in_=b_bf[:])
 
-        def z_views(r):
-            half = slice(2 * R * (r // 2), 2 * R * (r // 2) + 2 * R)
-            dst = z_bf[r % 2][half, :].rearrange("p (k t) -> p k t", t=T)
-            src = z_ps[r][half, :].rearrange("p (t k) -> p k t", t=T)
+        def z_views(m):
+            dst = z_bf[m][:].rearrange("p (k t) -> p k t", t=T)
+            src = z_ps[m][:].rearrange("p (t k) -> p k t", t=T)
             return dst, src
 
-        banks = [w_ps, z_ps]
+        dst, src = z_views(0)
+        nc.scalar.copy(out=dst, in_=src)
+        dst, src = z_views(1)
+        nc.vector.tensor_copy(out=dst, in_=src)
         for m in range(2):
-            dst, src = z_views(m)
-            nc.scalar.copy(out=dst, in_=src)
-            dst, src = z_views(2 + m)
-            nc.vector.tensor_copy(out=dst, in_=src)
             nc.vector.quantize_mx(out=z_codes[m][:].bitcast(FP8X4), scales=z_scales[m][:], in_=z_bf[m][:])
             for r in range(4):
                 rows = slice(R * r, R * r + R)
                 nc.tensor.matmul_mx(
-                    out=banks[m][r][:, :L],
+                    out=w_ps[r, m][:, :L],
                     lhsT=z_codes[m][rows, :].bitcast(FP8X4),
                     lhsT_scale=z_scales[m][rows, :],
                     rhs=b_codes[rows, :].bitcast(FP8X4),
@@ -126,26 +136,26 @@ def tile_rows_kron_soft_kernel(tc, x, a, b, th, out):
                     stop=True,
                 )
 
+        y = [sb.tile([P, L], F32, name="y%d" % g) for g in range(G)]
+        up = [sb.tile([P, L], F32, name="up%d" % g) for g in range(G)]
+        down = [sb.tile([P, L], F32, name="down%d" % i) for i in range(4)]
+
         for m in range(2):
-            y_s = sb.tile([P, 2, L], F32, name="y_s%d" % m)
-            y_v = sb.tile([P, 2, L], F32, name="y_v%d" % m)
-            up = [sb.tile([P, L], F32, name="up%d_%d" % (m, i)) for i in range(4)]
-            down = [sb.tile([P, L], F32, name="down%d_%d" % (m, i)) for i in range(2)]
-            for i in range(2):
-                w = banks[m][2 * i][:, :L]
-                nc.scalar.activation(out=up[i][:], in_=w, func=ACT.Relu, bias=th_neg[:], scale=1.0)
-                nc.scalar.activation(out=down[i][:], in_=w, func=ACT.Relu, bias=th_neg[:], scale=-1.0)
-                nc.gpsimd.tensor_tensor(out=y_s[:, i, :], in0=up[i][:], in1=down[i][:], op=ALU.subtract)
-            for i in range(2):
-                nc.vector.tensor_scalar(up[2 + i][:], banks[m][2 * i + 1][:, :L], th_pos[:], None, op0=ALU.max)
-            for i in range(2):
+            for r in (1, 3):
+                nc.vector.tensor_scalar(up[2 * r + m][:], w_ps[r, m][:, :L], th_pos[:], None, op0=ALU.max)
+            for r in (1, 3):
+                g = 2 * r + m
                 nc.vector.scalar_tensor_tensor(
-                    out=y_v[:, i, :],
-                    in0=banks[m][2 * i + 1][:, :L],
-                    scalar=th_neg[:],
-                    in1=up[2 + i][:],
-                    op0=ALU.min,
-                    op1=ALU.add,
+                    out=y[g][:], in0=w_ps[r, m][:, :L], scalar=th_neg[:], in1=up[g][:], op0=ALU.min, op1=ALU.add
                 )
-            nc.sync.dma_start(out=out[4 + m : 8 : 2].rearrange("g k l -> k g l"), in_=y_v[:])
-            nc.sync.dma_start(out=out[m:4:2].rearrange("g k l -> k g l"), in_=y_s[:])
+            for r in (0, 2):
+                g = 2 * r + m
+                w = w_ps[r, m][:, :L]
+                nc.scalar.activation(out=up[g][:], in_=w, func=ACT.Relu, bias=th_neg[:], scale=1.0)
+                nc.scalar.activation(out=down[r + m][:], in_=w, func=ACT.Relu, bias=th_neg[:], scale=-1.0)
+                last = m == 1 and r == 2
+                (nc.vector if last else nc.gpsimd).tensor_tensor(
+                    out=y[g][:], in0=up[g][:], in1=down[r + m][:], op=ALU.subtract
+                )
+            for r in (1, 0, 3, 2):
+                nc.sync.dma_start(out=out[2 * r + m], in_=y[2 * r + m][:])

@@ -9,6 +9,7 @@ F32 = mybir.dt.float32
 BF16 = mybir.dt.bfloat16
 U32 = mybir.dt.uint32
 U8 = mybir.dt.uint8
+I32 = mybir.dt.int32
 FP8X4 = mybir.dt.float8_e4m3fn_x4
 ALU = mybir.AluOpType
 ACT = mybir.ActivationFunctionType
@@ -17,7 +18,7 @@ P = 128
 R = 32
 T = 4
 TOP = 3 * R
-LAST_SCALAR = 10
+LAST_SCALAR = 20
 
 
 def tile_rows_kron_soft_kernel(tc, x, a, b, th, out):
@@ -28,19 +29,15 @@ def tile_rows_kron_soft_kernel(tc, x, a, b, th, out):
         ctx.enter_context(tc.manual_schedule())
 
         x_raw = [sb.tile([P, T * J], F32, name="x_raw%d" % i) for i in range(4)]
-        a_raw = sb.tile([P, T * K], F32)
-        b_raw = sb.tile([P, T * L], F32)
+        ab_raw = sb.tile([P, T * K], F32)
         th_pos = sb.tile([P, 1], F32)
         th_neg = sb.tile([P, 1], F32)
         x_bf = sb.tile([P, T * T * J], BF16, align_bytes=64)
-        a_bf = sb.tile([P, T * K], BF16, align_bytes=64)
-        b_bf = sb.tile([P, T * L], BF16, align_bytes=64)
+        ab_bf = sb.tile([P, T * K], BF16, align_bytes=64)
         x_codes = [sb.tile([P, J], U32, align_bytes=64, name="x_codes%d" % t) for t in range(T)]
         x_scales = [sb.tile([P, J], U8, align_bytes=64, name="x_scales%d" % t) for t in range(T)]
-        a_codes = sb.tile([P, K], U32, align_bytes=64)
-        a_scales = sb.tile([P, K], U8, align_bytes=64)
-        b_codes = sb.tile([P, L], U32, align_bytes=64)
-        b_scales = sb.tile([P, L], U8, align_bytes=64)
+        ab_mx = sb.tile([P, K + K // 4], U32, align_bytes=64)
+        b_mx = sb.tile([P, L + L // 4], U32, align_bytes=64)
         z_bf = [sb.tile([P, T * K], BF16, align_bytes=64, name="z_bf%d" % m) for m in range(2)]
         z_codes = [sb.tile([P, K], U32, align_bytes=64, name="z_codes%d" % m) for m in range(2)]
         z_scales = [sb.tile([P, K], U8, align_bytes=64, name="z_scales%d" % m) for m in range(2)]
@@ -53,46 +50,51 @@ def tile_rows_kron_soft_kernel(tc, x, a, b, th, out):
                 else:
                     w_ps[r, m] = ps.tile([P, L], F32, name="w_ps%d_%d" % (r, m))
 
-        nc.scalar.dma_start(out=th_pos[:], in_=th)
-        for r in (1, 2):
-            nc.sync.dma_start(out=a_raw[R * r : R * r + R, :], in_=a.rearrange("(q s) c -> q (s c)", s=T))
+        for r, src in ((1, a), (2, a), (0, b)):
+            nc.sync.dma_start(out=ab_raw[R * r : R * r + R, :], in_=src.rearrange("(q s) c -> q (s c)", s=T))
         for i in range(4):
             nc.sync.dma_start(
                 out=x_raw[i][R:TOP, :], in_=x[2 * i : 2 * i + 2].rearrange("g (q s) j -> (g q) (s j)", s=T)
             )
-        for r in (0, 2, 1, 3):
-            nc.sync.dma_start(out=b_raw[R * r : R * r + R, :], in_=b.rearrange("(q s) c -> q (s c)", s=T))
+        nc.sync.dma_start(out=th_pos[:], in_=th)
 
-        nc.scalar.mul(th_neg[:], th_pos[:], -1.0)
-        nc.vector.memset(a_raw[:R, :], 0.0)
+        nc.gpsimd.memset(x_raw[2][:R, :], 0.0)
+        nc.scalar.copy(out=x_raw[3][:R, :], in_=x_raw[2][:R, :])
+        nc.vector.memset(ab_mx[:, K:].bitcast(I32), 0)
         for i in range(2):
             nc.vector.memset(x_raw[i][:R, :], 0.0)
-            nc.gpsimd.memset(x_raw[2 + i][:R, :], 0.0)
+        nc.gpsimd.tensor_scalar(th_neg[:], th_pos[:], -1.0, 0.0, op0=ALU.mult, op1=ALU.add)
 
-        def x_views(i):
-            dst = x_bf[:TOP, :].rearrange("p (t i u s) -> p i u s t", t=T, i=4, s=T)[:, i]
-            src = x_raw[i][:TOP, :].rearrange("p (s u t) -> p u s t", s=T, t=T)
+        def codes(mx, rows):
+            return mx[rows, :P].bitcast(FP8X4)
+
+        def scales(mx, rows):
+            return mx[rows, P:].bitcast(U8)
+
+        def x_views(i, pair):
+            ts = slice(2 * pair, 2 * pair + 2)
+            dst = x_bf[:TOP, :].rearrange("p (t i u s) -> p i u s t", t=T, i=4, s=T)[:, i, :, :, ts]
+            src = x_raw[i][:TOP, :].rearrange("p (s u t) -> p u s t", s=T, t=T)[:, :, :, ts]
             return dst, src
 
-        def factor_views(bf, raw):
-            dst = bf.rearrange("p (c i s) -> p c s i", i=4, s=T)
-            src = raw.rearrange("p (s c i) -> p c s i", s=T, i=4)
-            return dst, src
+        top = slice(0, TOP)
+        nc.vector.tensor_copy(
+            out=ab_bf[top, :].rearrange("p (c i s) -> p c s i", i=4, s=T),
+            in_=ab_raw[top, :].rearrange("p (s c i) -> p c s i", s=T, i=4),
+        )
+        nc.vector.quantize_mx(out=codes(ab_mx, top), scales=scales(ab_mx, top), in_=ab_bf[top, :])
+        for r in (1, 2, 3):
+            nc.sync.dma_start(out=b_mx[R * r : R * r + R, :].bitcast(I32), in_=ab_mx[:R, :].bitcast(I32))
 
-        dst, src = factor_views(a_bf[:TOP, :], a_raw[:TOP, :])
-        nc.scalar.copy(out=dst, in_=src)
-        dst, src = x_views(0)
-        nc.vector.tensor_copy(out=dst, in_=src)
-        dst, src = x_views(1)
-        nc.scalar.copy(out=dst, in_=src)
-        dst, src = x_views(2)
-        nc.vector.tensor_copy(out=dst, in_=src)
-        dst, src = x_views(3)
+        for i, pair in ((0, 0), (0, 1), (2, 1)):
+            dst, src = x_views(i, pair)
+            nc.scalar.copy(out=dst, in_=src)
+        for i, pair in ((1, 0), (1, 1), (2, 0), (3, 0)):
+            dst, src = x_views(i, pair)
+            nc.vector.tensor_copy(out=dst, in_=src)
+        dst, src = x_views(3, 1)
         nc.scalar.copy(out=dst[:, :LAST_SCALAR], in_=src[:, :LAST_SCALAR])
         nc.vector.tensor_copy(out=dst[:, LAST_SCALAR:], in_=src[:, LAST_SCALAR:])
-        nc.vector.quantize_mx(out=a_codes[:TOP, :].bitcast(FP8X4), scales=a_scales[:TOP, :], in_=a_bf[:TOP, :])
-        dst, src = factor_views(b_bf[:], b_raw[:])
-        nc.scalar.copy(out=dst, in_=src)
 
         for t in range(T):
             nc.vector.quantize_mx(
@@ -106,12 +108,11 @@ def tile_rows_kron_soft_kernel(tc, x, a, b, th, out):
                     out=z_ps[m][:, K * t : K * t + K],
                     lhsT=x_codes[t][rows, :].bitcast(FP8X4),
                     lhsT_scale=x_scales[t][rows, :],
-                    rhs=a_codes[rows, :].bitcast(FP8X4),
-                    rhs_scale=a_scales[rows, :],
+                    rhs=codes(ab_mx, rows),
+                    rhs_scale=scales(ab_mx, rows),
                     start=True,
                     stop=True,
                 )
-        nc.vector.quantize_mx(out=b_codes[:].bitcast(FP8X4), scales=b_scales[:], in_=b_bf[:])
 
         def z_views(m):
             dst = z_bf[m][:].rearrange("p (k t) -> p k t", t=T)
@@ -130,8 +131,8 @@ def tile_rows_kron_soft_kernel(tc, x, a, b, th, out):
                     out=w_ps[r, m][:, :L],
                     lhsT=z_codes[m][rows, :].bitcast(FP8X4),
                     lhsT_scale=z_scales[m][rows, :],
-                    rhs=b_codes[rows, :].bitcast(FP8X4),
-                    rhs_scale=b_scales[rows, :],
+                    rhs=codes(b_mx if r else ab_mx, rows),
+                    rhs_scale=scales(b_mx if r else ab_mx, rows),
                     start=True,
                     stop=True,
                 )

@@ -18,7 +18,7 @@ P = 128
 R = 32
 T = 4
 TOP = 3 * R
-LAST_SCALAR = 20
+LAST_SCALAR = 12
 
 
 def tile_rows_kron_soft_kernel(tc, x, a, b, th, out):
@@ -56,14 +56,12 @@ def tile_rows_kron_soft_kernel(tc, x, a, b, th, out):
             nc.sync.dma_start(
                 out=x_raw[i][R:TOP, :], in_=x[2 * i : 2 * i + 2].rearrange("g (q s) j -> (g q) (s j)", s=T)
             )
-        nc.sync.dma_start(out=th_pos[:], in_=th)
 
         nc.gpsimd.memset(x_raw[2][:R, :], 0.0)
         nc.scalar.copy(out=x_raw[3][:R, :], in_=x_raw[2][:R, :])
         nc.vector.memset(ab_mx[:, K:].bitcast(I32), 0)
         for i in range(2):
             nc.vector.memset(x_raw[i][:R, :], 0.0)
-        nc.gpsimd.tensor_scalar(th_neg[:], th_pos[:], -1.0, 0.0, op0=ALU.mult, op1=ALU.add)
 
         def codes(mx, rows):
             return mx[rows, :P].bitcast(FP8X4)
@@ -85,16 +83,20 @@ def tile_rows_kron_soft_kernel(tc, x, a, b, th, out):
         nc.vector.quantize_mx(out=codes(ab_mx, top), scales=scales(ab_mx, top), in_=ab_bf[top, :])
         for r in (1, 2, 3):
             nc.sync.dma_start(out=b_mx[R * r : R * r + R, :].bitcast(I32), in_=ab_mx[:R, :].bitcast(I32))
+        nc.sync.dma_start(out=th_pos[:], in_=th)
+        nc.gpsimd.tensor_scalar(th_neg[:], th_pos[:], -1.0, 0.0, op0=ALU.mult, op1=ALU.add)
 
         for i, pair in ((0, 0), (0, 1), (2, 1)):
             dst, src = x_views(i, pair)
             nc.scalar.copy(out=dst, in_=src)
-        for i, pair in ((1, 0), (1, 1), (2, 0), (3, 0)):
+        for i, pair in ((1, 0), (1, 1), (2, 0)):
             dst, src = x_views(i, pair)
             nc.vector.tensor_copy(out=dst, in_=src)
-        dst, src = x_views(3, 1)
+        dst, src = x_views(3, 0)
         nc.scalar.copy(out=dst[:, :LAST_SCALAR], in_=src[:, :LAST_SCALAR])
         nc.vector.tensor_copy(out=dst[:, LAST_SCALAR:], in_=src[:, LAST_SCALAR:])
+        dst, src = x_views(3, 1)
+        nc.vector.tensor_copy(out=dst, in_=src)
 
         for t in range(T):
             nc.vector.quantize_mx(
@@ -139,24 +141,23 @@ def tile_rows_kron_soft_kernel(tc, x, a, b, th, out):
 
         y = [sb.tile([P, L], F32, name="y%d" % g) for g in range(G)]
         up = [sb.tile([P, L], F32, name="up%d" % g) for g in range(G)]
-        down = [sb.tile([P, L], F32, name="down%d" % i) for i in range(4)]
 
-        for m in range(2):
-            for r in (1, 3):
-                nc.vector.tensor_scalar(up[2 * r + m][:], w_ps[r, m][:, :L], th_pos[:], None, op0=ALU.max)
-            for r in (1, 3):
-                g = 2 * r + m
+        def w_of(g):
+            return w_ps[g // 2, g % 2][:, :L]
+
+        down = {g: sb.tile([P, L], F32, name="down%d" % g) for g in (0, 4, 1)}
+        for g in (0, 4, 1):
+            nc.scalar.activation(out=up[g][:], in_=w_of(g), func=ACT.Relu, bias=th_neg[:], scale=1.0)
+            nc.scalar.activation(out=down[g][:], in_=w_of(g), func=ACT.Relu, bias=th_neg[:], scale=-1.0)
+        for g in (0, 4):
+            nc.gpsimd.tensor_tensor(out=y[g][:], in0=up[g][:], in1=down[g][:], op=ALU.subtract)
+        for batch in ((2, 6), (3, 5, 7)):
+            for g in batch:
+                nc.vector.tensor_scalar(up[g][:], w_of(g), th_pos[:], None, op0=ALU.max)
+            for g in batch:
                 nc.vector.scalar_tensor_tensor(
-                    out=y[g][:], in0=w_ps[r, m][:, :L], scalar=th_neg[:], in1=up[g][:], op0=ALU.min, op1=ALU.add
+                    out=y[g][:], in0=w_of(g), scalar=th_neg[:], in1=up[g][:], op0=ALU.min, op1=ALU.add
                 )
-            for r in (0, 2):
-                g = 2 * r + m
-                w = w_ps[r, m][:, :L]
-                nc.scalar.activation(out=up[g][:], in_=w, func=ACT.Relu, bias=th_neg[:], scale=1.0)
-                nc.scalar.activation(out=down[r + m][:], in_=w, func=ACT.Relu, bias=th_neg[:], scale=-1.0)
-                last = m == 1 and r == 2
-                (nc.vector if last else nc.gpsimd).tensor_tensor(
-                    out=y[g][:], in0=up[g][:], in1=down[r + m][:], op=ALU.subtract
-                )
-            for r in (1, 0, 3, 2):
-                nc.sync.dma_start(out=out[2 * r + m], in_=y[2 * r + m][:])
+        nc.vector.tensor_tensor(out=y[1][:], in0=up[1][:], in1=down[1][:], op=ALU.subtract)
+        for g in (2, 6, 0, 3, 5, 4, 7, 1):
+            nc.sync.dma_start(out=out[g], in_=y[g][:])

@@ -18,7 +18,8 @@ P = 128
 R = 32
 T = 4
 TOP = 3 * R
-LAST_SCALAR = 12
+AB_SCALAR = 10
+LAST_SCALAR = 20
 
 
 def tile_rows_kron_soft_kernel(tc, x, a, b, th, out):
@@ -76,27 +77,27 @@ def tile_rows_kron_soft_kernel(tc, x, a, b, th, out):
             return dst, src
 
         top = slice(0, TOP)
-        nc.vector.tensor_copy(
-            out=ab_bf[top, :].rearrange("p (c i s) -> p c s i", i=4, s=T),
-            in_=ab_raw[top, :].rearrange("p (s c i) -> p c s i", s=T, i=4),
-        )
+        dst = ab_bf[top, :].rearrange("p (c i s) -> p c s i", i=4, s=T)
+        src = ab_raw[top, :].rearrange("p (s c i) -> p c s i", s=T, i=4)
+        nc.scalar.copy(out=dst[:, :AB_SCALAR], in_=src[:, :AB_SCALAR])
+        nc.vector.tensor_copy(out=dst[:, AB_SCALAR:], in_=src[:, AB_SCALAR:])
+        dst, src = x_views(0, 0)
+        nc.vector.tensor_copy(out=dst, in_=src)
         nc.vector.quantize_mx(out=codes(ab_mx, top), scales=scales(ab_mx, top), in_=ab_bf[top, :])
         for r in (1, 2, 3):
             nc.sync.dma_start(out=b_mx[R * r : R * r + R, :].bitcast(I32), in_=ab_mx[:R, :].bitcast(I32))
         nc.sync.dma_start(out=th_pos[:], in_=th)
         nc.gpsimd.tensor_scalar(th_neg[:], th_pos[:], -1.0, 0.0, op0=ALU.mult, op1=ALU.add)
 
-        for i, pair in ((0, 0), (0, 1), (2, 1)):
-            dst, src = x_views(i, pair)
-            nc.scalar.copy(out=dst, in_=src)
-        for i, pair in ((1, 0), (1, 1), (2, 0)):
-            dst, src = x_views(i, pair)
+        for i in range(1, 4):
+            dst, src = x_views(i, 0)
             nc.vector.tensor_copy(out=dst, in_=src)
-        dst, src = x_views(3, 0)
+        for i in range(3):
+            dst, src = x_views(i, 1)
+            nc.scalar.copy(out=dst, in_=src)
+        dst, src = x_views(3, 1)
         nc.scalar.copy(out=dst[:, :LAST_SCALAR], in_=src[:, :LAST_SCALAR])
         nc.vector.tensor_copy(out=dst[:, LAST_SCALAR:], in_=src[:, LAST_SCALAR:])
-        dst, src = x_views(3, 1)
-        nc.vector.tensor_copy(out=dst, in_=src)
 
         for t in range(T):
             nc.vector.quantize_mx(
@@ -127,7 +128,7 @@ def tile_rows_kron_soft_kernel(tc, x, a, b, th, out):
         nc.vector.tensor_copy(out=dst, in_=src)
         for m in range(2):
             nc.vector.quantize_mx(out=z_codes[m][:].bitcast(FP8X4), scales=z_scales[m][:], in_=z_bf[m][:])
-            for r in range(4):
+            for r in (1, 0, 3, 2):
                 rows = slice(R * r, R * r + R)
                 nc.tensor.matmul_mx(
                     out=w_ps[r, m][:, :L],
@@ -151,7 +152,7 @@ def tile_rows_kron_soft_kernel(tc, x, a, b, th, out):
             nc.scalar.activation(out=down[g][:], in_=w_of(g), func=ACT.Relu, bias=th_neg[:], scale=-1.0)
         for g in (0, 4):
             nc.gpsimd.tensor_tensor(out=y[g][:], in0=up[g][:], in1=down[g][:], op=ALU.subtract)
-        for batch in ((2, 6), (3, 5, 7)):
+        for batch in ((2, 6), (3, 7, 5)):
             for g in batch:
                 nc.vector.tensor_scalar(up[g][:], w_of(g), th_pos[:], None, op0=ALU.max)
             for g in batch:
@@ -159,5 +160,5 @@ def tile_rows_kron_soft_kernel(tc, x, a, b, th, out):
                     out=y[g][:], in0=w_of(g), scalar=th_neg[:], in1=up[g][:], op0=ALU.min, op1=ALU.add
                 )
         nc.vector.tensor_tensor(out=y[1][:], in0=up[1][:], in1=down[1][:], op=ALU.subtract)
-        for g in (2, 6, 0, 3, 5, 4, 7, 1):
+        for g in (2, 6, 0, 3, 7, 4, 5, 1):
             nc.sync.dma_start(out=out[g], in_=y[g][:])

@@ -31,8 +31,8 @@ def tile_rows_kron_soft_kernel(tc, x, a, b, th, out):
 
         x_raw = [sb.tile([P, T * J], F32, name="x_raw%d" % i) for i in range(4)]
         ab_raw = sb.tile([P, T * K], F32)
-        th_pos = sb.tile([P, 1], F32)
-        th_neg = sb.tile([P, 1], F32)
+        th_pos = sb.tile([P, 2], F32)
+        th_neg = sb.tile([P, 2], F32)
         x_bf = sb.tile([P, T * T * J], BF16, align_bytes=64)
         ab_bf = sb.tile([P, T * K], BF16, align_bytes=64)
         x_codes = [sb.tile([P, J], U32, align_bytes=64, name="x_codes%d" % t) for t in range(T)]
@@ -86,7 +86,8 @@ def tile_rows_kron_soft_kernel(tc, x, a, b, th, out):
         nc.vector.quantize_mx(out=codes(ab_mx, top), scales=scales(ab_mx, top), in_=ab_bf[top, :])
         for r in (1, 2, 3):
             nc.sync.dma_start(out=b_mx[R * r : R * r + R, :].bitcast(I32), in_=ab_mx[:R, :].bitcast(I32))
-        nc.sync.dma_start(out=th_pos[:], in_=th)
+        for m in range(2):
+            nc.sync.dma_start(out=th_pos[64 * m : 64 * m + 64, :], in_=th.rearrange("(h e) o -> h (e o)", e=2))
         nc.gpsimd.tensor_scalar(th_neg[:], th_pos[:], -1.0, 0.0, op0=ALU.mult, op1=ALU.add)
 
         for i in range(1, 4):
@@ -117,48 +118,63 @@ def tile_rows_kron_soft_kernel(tc, x, a, b, th, out):
                     stop=True,
                 )
 
-        def z_views(m):
-            dst = z_bf[m][:].rearrange("p (k t) -> p k t", t=T)
-            src = z_ps[m][:].rearrange("p (t k) -> p k t", t=T)
+        def z_views(m, e):
+            dst = z_bf[e][:].rearrange("p (m h t) -> p m h t", m=2, t=T)[:, m]
+            src = z_ps[m][:].rearrange("p (t h e) -> p e h t", t=T, e=2)[:, e]
             return dst, src
 
-        dst, src = z_views(0)
-        nc.scalar.copy(out=dst, in_=src)
-        dst, src = z_views(1)
-        nc.vector.tensor_copy(out=dst, in_=src)
-        for m in range(2):
-            nc.vector.quantize_mx(out=z_codes[m][:].bitcast(FP8X4), scales=z_scales[m][:], in_=z_bf[m][:])
-            for r in (1, 0, 3, 2):
+        for e in range(2):
+            dst, src = z_views(0, e)
+            nc.scalar.copy(out=dst, in_=src)
+            dst, src = z_views(1, e)
+            nc.vector.tensor_copy(out=dst, in_=src)
+        for e in range(2):
+            nc.vector.quantize_mx(out=z_codes[e][:].bitcast(FP8X4), scales=z_scales[e][:], in_=z_bf[e][:])
+            for r in (0, 1, 3, 2):
                 rows = slice(R * r, R * r + R)
                 nc.tensor.matmul_mx(
-                    out=w_ps[r, m][:, :L],
-                    lhsT=z_codes[m][rows, :].bitcast(FP8X4),
-                    lhsT_scale=z_scales[m][rows, :],
+                    out=w_ps[r, e][:, :L],
+                    lhsT=z_codes[e][rows, :].bitcast(FP8X4),
+                    lhsT_scale=z_scales[e][rows, :],
                     rhs=codes(b_mx if r else ab_mx, rows),
                     rhs_scale=scales(b_mx if r else ab_mx, rows),
                     start=True,
                     stop=True,
                 )
 
-        y = [sb.tile([P, L], F32, name="y%d" % g) for g in range(G)]
-        up = [sb.tile([P, L], F32, name="up%d" % g) for g in range(G)]
+        y = [sb.tile([P, 2, L], F32, name="y%d" % r) for r in range(4)]
+        up = {(r, e): sb.tile([P, L], F32, name="up%d_%d" % (r, e)) for r in range(4) for e in range(2)}
+        down = {(r, e): sb.tile([P, L], F32, name="down%d_%d" % (r, e)) for r in (0, 3) for e in range(2)}
 
-        def w_of(g):
-            return w_ps[g // 2, g % 2][:, :L]
+        def w_of(r, e):
+            return w_ps[r, e][:, :L]
 
-        down = {g: sb.tile([P, L], F32, name="down%d" % g) for g in (0, 4, 1)}
-        for g in (0, 4, 1):
-            nc.scalar.activation(out=up[g][:], in_=w_of(g), func=ACT.Relu, bias=th_neg[:], scale=1.0)
-            nc.scalar.activation(out=down[g][:], in_=w_of(g), func=ACT.Relu, bias=th_neg[:], scale=-1.0)
-        for g in (0, 4):
-            nc.gpsimd.tensor_tensor(out=y[g][:], in0=up[g][:], in1=down[g][:], op=ALU.subtract)
-        for batch in ((2, 6), (3, 7, 5)):
-            for g in batch:
-                nc.vector.tensor_scalar(up[g][:], w_of(g), th_pos[:], None, op0=ALU.max)
-            for g in batch:
+        def store(r):
+            nc.sync.dma_start(
+                out=out[2 * r : 2 * r + 2].rearrange("m (h e) l -> (m h) (e l)", e=2),
+                in_=y[r][:].rearrange("p e l -> p (e l)"),
+            )
+
+        for r in (0, 3):
+            for e in range(2):
+                bias = th_neg[:, e : e + 1]
+                nc.scalar.activation(out=up[r, e][:], in_=w_of(r, e), func=ACT.Relu, bias=bias, scale=1.0)
+                nc.scalar.activation(out=down[r, e][:], in_=w_of(r, e), func=ACT.Relu, bias=bias, scale=-1.0)
+        for e in range(2):
+            nc.gpsimd.tensor_tensor(out=y[0][:, e, :], in0=up[0, e][:], in1=down[0, e][:], op=ALU.subtract)
+        for r in (1, 2):
+            for e in range(2):
+                nc.vector.tensor_scalar(up[r, e][:], w_of(r, e), th_pos[:, e : e + 1], None, op0=ALU.max)
+            for e in range(2):
                 nc.vector.scalar_tensor_tensor(
-                    out=y[g][:], in0=w_of(g), scalar=th_neg[:], in1=up[g][:], op0=ALU.min, op1=ALU.add
+                    out=y[r][:, e, :],
+                    in0=w_of(r, e),
+                    scalar=th_neg[:, e : e + 1],
+                    in1=up[r, e][:],
+                    op0=ALU.min,
+                    op1=ALU.add,
                 )
-        nc.vector.tensor_tensor(out=y[1][:], in0=up[1][:], in1=down[1][:], op=ALU.subtract)
-        for g in (2, 6, 0, 3, 7, 4, 5, 1):
-            nc.sync.dma_start(out=out[g], in_=y[g][:])
+        for e in range(2):
+            nc.vector.tensor_tensor(out=y[3][:, e, :], in0=up[3, e][:], in1=down[3, e][:], op=ALU.subtract)
+        for r in (1, 0, 2, 3):
+            store(r)

@@ -9,7 +9,6 @@ F32 = mybir.dt.float32
 BF16 = mybir.dt.bfloat16
 U32 = mybir.dt.uint32
 U8 = mybir.dt.uint8
-I32 = mybir.dt.int32
 FP8X4 = mybir.dt.float8_e4m3fn_x4
 ALU = mybir.AluOpType
 ACT = mybir.ActivationFunctionType
@@ -31,6 +30,8 @@ def tile_rows_kron_soft_kernel(tc, x, a, b, th, out):
 
         x_raw = [sb.tile([P, T * J], F32, name="x_raw%d" % i) for i in range(4)]
         ab_raw = sb.tile([P, T * K], F32)
+        b_raw = sb.tile([P, T * L], F32)
+        b_bf = sb.tile([P, T * L], BF16, align_bytes=64)
         th_pos = sb.tile([P, 2], F32)
         th_neg = sb.tile([P, 2], F32)
         x_bf = sb.tile([P, T * T * J], BF16, align_bytes=64)
@@ -51,16 +52,20 @@ def tile_rows_kron_soft_kernel(tc, x, a, b, th, out):
                 else:
                     w_ps[r, m] = ps.tile([P, L], F32, name="w_ps%d_%d" % (r, m))
 
-        for r, src in ((1, a), (2, a), (0, b)):
-            nc.sync.dma_start(out=ab_raw[R * r : R * r + R, :], in_=src.rearrange("(q s) c -> q (s c)", s=T))
+        for r in (1, 2):
+            nc.sync.dma_start(out=ab_raw[R * r : R * r + R, :], in_=a.rearrange("(q s) c -> q (s c)", s=T))
         for i in range(4):
             nc.sync.dma_start(
                 out=x_raw[i][R:TOP, :], in_=x[2 * i : 2 * i + 2].rearrange("g (q s) j -> (g q) (s j)", s=T)
             )
+        for r in (0, 2, 1, 3):
+            nc.sync.dma_start(out=b_raw[R * r : R * r + R, :], in_=b.rearrange("(q s) c -> q (s c)", s=T))
+        for m in range(2):
+            nc.sync.dma_start(out=th_pos[64 * m : 64 * m + 64, :], in_=th.rearrange("(h e) o -> h (e o)", e=2))
 
         nc.gpsimd.memset(x_raw[2][:R, :], 0.0)
         nc.scalar.copy(out=x_raw[3][:R, :], in_=x_raw[2][:R, :])
-        nc.vector.memset(ab_mx[:, K:].bitcast(I32), 0)
+        nc.vector.memset(ab_raw[:R, :], 0.0)
         for i in range(2):
             nc.vector.memset(x_raw[i][:R, :], 0.0)
 
@@ -84,11 +89,6 @@ def tile_rows_kron_soft_kernel(tc, x, a, b, th, out):
         dst, src = x_views(0, 0)
         nc.vector.tensor_copy(out=dst, in_=src)
         nc.vector.quantize_mx(out=codes(ab_mx, top), scales=scales(ab_mx, top), in_=ab_bf[top, :])
-        for r in (1, 2, 3):
-            nc.sync.dma_start(out=b_mx[R * r : R * r + R, :].bitcast(I32), in_=ab_mx[:R, :].bitcast(I32))
-        for m in range(2):
-            nc.sync.dma_start(out=th_pos[64 * m : 64 * m + 64, :], in_=th.rearrange("(h e) o -> h (e o)", e=2))
-        nc.gpsimd.tensor_scalar(th_neg[:], th_pos[:], -1.0, 0.0, op0=ALU.mult, op1=ALU.add)
 
         for i in range(1, 4):
             dst, src = x_views(i, 0)
@@ -99,6 +99,12 @@ def tile_rows_kron_soft_kernel(tc, x, a, b, th, out):
         dst, src = x_views(3, 1)
         nc.scalar.copy(out=dst[:, :LAST_SCALAR], in_=src[:, :LAST_SCALAR])
         nc.vector.tensor_copy(out=dst[:, LAST_SCALAR:], in_=src[:, LAST_SCALAR:])
+
+        nc.scalar.copy(
+            out=b_bf[:].rearrange("p (c i s) -> p c s i", i=4, s=T),
+            in_=b_raw[:].rearrange("p (s c i) -> p c s i", s=T, i=4),
+        )
+        nc.scalar.mul(th_neg[:], th_pos[:], -1.0)
 
         for t in range(T):
             nc.vector.quantize_mx(
@@ -118,6 +124,8 @@ def tile_rows_kron_soft_kernel(tc, x, a, b, th, out):
                     stop=True,
                 )
 
+        nc.vector.quantize_mx(out=codes(b_mx, slice(0, P)), scales=scales(b_mx, slice(0, P)), in_=b_bf[:])
+
         def z_views(m, e):
             dst = z_bf[e][:].rearrange("p (m h t) -> p m h t", m=2, t=T)[:, m]
             src = z_ps[m][:].rearrange("p (t h e) -> p e h t", t=T, e=2)[:, e]
@@ -136,8 +144,8 @@ def tile_rows_kron_soft_kernel(tc, x, a, b, th, out):
                     out=w_ps[r, e][:, :L],
                     lhsT=z_codes[e][rows, :].bitcast(FP8X4),
                     lhsT_scale=z_scales[e][rows, :],
-                    rhs=codes(b_mx if r else ab_mx, rows),
-                    rhs_scale=scales(b_mx if r else ab_mx, rows),
+                    rhs=codes(b_mx, rows),
+                    rhs_scale=scales(b_mx, rows),
                     start=True,
                     stop=True,
                 )

@@ -19,6 +19,7 @@ T = 4
 TOP = 3 * R
 AB_SCALAR = 10
 LAST_SCALAR = 20
+B_SCALAR = 16
 
 
 def tile_rows_kron_soft_kernel(tc, x, a, b, th, out):
@@ -100,11 +101,9 @@ def tile_rows_kron_soft_kernel(tc, x, a, b, th, out):
         nc.scalar.copy(out=dst[:, :LAST_SCALAR], in_=src[:, :LAST_SCALAR])
         nc.vector.tensor_copy(out=dst[:, LAST_SCALAR:], in_=src[:, LAST_SCALAR:])
 
-        nc.scalar.copy(
-            out=b_bf[:].rearrange("p (c i s) -> p c s i", i=4, s=T),
-            in_=b_raw[:].rearrange("p (s c i) -> p c s i", s=T, i=4),
-        )
-        nc.scalar.mul(th_neg[:], th_pos[:], -1.0)
+        b_dst = b_bf[:].rearrange("p (c i s) -> p c s i", i=4, s=T)
+        b_src = b_raw[:].rearrange("p (s c i) -> p c s i", s=T, i=4)
+        nc.scalar.copy(out=b_dst[:, :B_SCALAR], in_=b_src[:, :B_SCALAR])
 
         for t in range(T):
             nc.vector.quantize_mx(
@@ -124,6 +123,7 @@ def tile_rows_kron_soft_kernel(tc, x, a, b, th, out):
                     stop=True,
                 )
 
+        nc.vector.tensor_copy(out=b_dst[:, B_SCALAR:], in_=b_src[:, B_SCALAR:])
         nc.vector.quantize_mx(out=codes(b_mx, slice(0, P)), scales=scales(b_mx, slice(0, P)), in_=b_bf[:])
 
         def z_views(m, e):
@@ -136,6 +136,7 @@ def tile_rows_kron_soft_kernel(tc, x, a, b, th, out):
             nc.scalar.copy(out=dst, in_=src)
             dst, src = z_views(1, e)
             nc.vector.tensor_copy(out=dst, in_=src)
+        nc.scalar.mul(th_neg[:], th_pos[:], -1.0)
         for e in range(2):
             nc.vector.quantize_mx(out=z_codes[e][:].bitcast(FP8X4), scales=z_scales[e][:], in_=z_bf[e][:])
             for r in (0, 1, 3, 2):
@@ -172,7 +173,9 @@ def tile_rows_kron_soft_kernel(tc, x, a, b, th, out):
             nc.gpsimd.tensor_tensor(out=y[0][:, e, :], in0=up[0, e][:], in1=down[0, e][:], op=ALU.subtract)
         for r in (1, 2):
             for e in range(2):
-                nc.vector.tensor_scalar(up[r, e][:], w_of(r, e), th_pos[:, e : e + 1], None, op0=ALU.max)
+                nc.vector.tensor_tensor(
+                    out=up[r, e][:], in0=w_of(r, e), in1=th_pos[:, e : e + 1].to_broadcast([P, L]), op=ALU.max
+                )
             for e in range(2):
                 nc.vector.scalar_tensor_tensor(
                     out=y[r][:, e, :],

@@ -9,6 +9,7 @@ F32 = mybir.dt.float32
 BF16 = mybir.dt.bfloat16
 U32 = mybir.dt.uint32
 U8 = mybir.dt.uint8
+I32 = mybir.dt.int32
 FP8X4 = mybir.dt.float8_e4m3fn_x4
 ALU = mybir.AluOpType
 ACT = mybir.ActivationFunctionType
@@ -20,6 +21,7 @@ TOP = 3 * R
 AB_SCALAR = 10
 LAST_SCALAR = 20
 B_SCALAR = 16
+FILL = 32
 
 
 def tile_rows_kron_soft_kernel(tc, x, a, b, th, out):
@@ -65,10 +67,11 @@ def tile_rows_kron_soft_kernel(tc, x, a, b, th, out):
             nc.sync.dma_start(out=th_pos[64 * m : 64 * m + 64, :], in_=th.rearrange("(h e) o -> h (e o)", e=2))
 
         nc.gpsimd.memset(x_raw[2][:R, :], 0.0)
-        nc.scalar.copy(out=x_raw[3][:R, :], in_=x_raw[2][:R, :])
-        nc.vector.memset(ab_raw[:R, :], 0.0)
+        nc.scalar.copy(out=x_raw[3][:R, :FILL], in_=x_raw[2][:R, :FILL])
+        nc.vector.memset(x_raw[3][:R, FILL:].bitcast(I32), 0)
         for i in range(2):
-            nc.vector.memset(x_raw[i][:R, :], 0.0)
+            nc.vector.memset(x_raw[i][:R, :].bitcast(I32), 0)
+        nc.vector.memset(ab_raw[:R, :].bitcast(I32), 0)
 
         def codes(mx, rows):
             return mx[rows, :P].bitcast(FP8X4)

@@ -129,6 +129,8 @@ def tile_rows_kron_soft_kernel(tc, x, a, b, th, out):
         nc.vector.tensor_copy(out=b_dst[:, B_SCALAR:], in_=b_src[:, B_SCALAR:])
         nc.vector.quantize_mx(out=codes(b_mx, slice(0, P)), scales=scales(b_mx, slice(0, P)), in_=b_bf[:])
 
+        nc.scalar.mul(th_neg[:], th_pos[:], -1.0)
+
         def z_views(m, e):
             dst = z_bf[e][:].rearrange("p (m h t) -> p m h t", m=2, t=T)[:, m]
             src = z_ps[m][:].rearrange("p (t h e) -> p e h t", t=T, e=2)[:, e]
@@ -139,7 +141,6 @@ def tile_rows_kron_soft_kernel(tc, x, a, b, th, out):
             nc.scalar.copy(out=dst, in_=src)
             dst, src = z_views(1, e)
             nc.vector.tensor_copy(out=dst, in_=src)
-        nc.scalar.mul(th_neg[:], th_pos[:], -1.0)
         for e in range(2):
             nc.vector.quantize_mx(out=z_codes[e][:].bitcast(FP8X4), scales=z_scales[e][:], in_=z_bf[e][:])
             for r in (0, 1, 3, 2):
@@ -172,23 +173,35 @@ def tile_rows_kron_soft_kernel(tc, x, a, b, th, out):
                 bias = th_neg[:, e : e + 1]
                 nc.scalar.activation(out=up[r, e][:], in_=w_of(r, e), func=ACT.Relu, bias=bias, scale=1.0)
                 nc.scalar.activation(out=down[r, e][:], in_=w_of(r, e), func=ACT.Relu, bias=bias, scale=-1.0)
-        for e in range(2):
-            nc.gpsimd.tensor_tensor(out=y[0][:, e, :], in0=up[0, e][:], in1=down[0, e][:], op=ALU.subtract)
-        for r in (1, 2):
-            for e in range(2):
-                nc.vector.tensor_tensor(
-                    out=up[r, e][:], in0=w_of(r, e), in1=th_pos[:, e : e + 1].to_broadcast([P, L]), op=ALU.max
-                )
-            for e in range(2):
-                nc.vector.scalar_tensor_tensor(
-                    out=y[r][:, e, :],
-                    in0=w_of(r, e),
-                    scalar=th_neg[:, e : e + 1],
-                    in1=up[r, e][:],
-                    op0=ALU.min,
-                    op1=ALU.add,
-                )
-        for e in range(2):
-            nc.vector.tensor_tensor(out=y[3][:, e, :], in0=up[3, e][:], in1=down[3, e][:], op=ALU.subtract)
+        def upper(r, e):
+            nc.vector.tensor_tensor(
+                out=up[r, e][:], in0=w_of(r, e), in1=th_pos[:, e : e + 1].to_broadcast([P, L]), op=ALU.max
+            )
+
+        def finish(r, e):
+            nc.vector.scalar_tensor_tensor(
+                out=y[r][:, e, :],
+                in0=w_of(r, e),
+                scalar=th_neg[:, e : e + 1],
+                in1=up[r, e][:],
+                op0=ALU.min,
+                op1=ALU.add,
+            )
+
+        def subtract(engine, r, e):
+            engine.tensor_tensor(out=y[r][:, e, :], in0=up[r, e][:], in1=down[r, e][:], op=ALU.subtract)
+
+        subtract(nc.gpsimd, 0, 0)
+        subtract(nc.gpsimd, 3, 0)
+        upper(1, 0)
+        upper(1, 1)
+        upper(2, 0)
+        finish(1, 0)
+        finish(1, 1)
+        upper(2, 1)
+        subtract(nc.vector, 0, 1)
+        finish(2, 0)
+        finish(2, 1)
+        subtract(nc.vector, 3, 1)
         for r in (1, 0, 2, 3):
             store(r)

@@ -19,7 +19,7 @@ R = 32
 T = 4
 TOP = 3 * R
 AB_SCALAR = 10
-LAST_SCALAR = 20
+LAST_SCALAR = 16
 B_SCALAR = 16
 FILL = 32
 
@@ -67,11 +67,10 @@ def tile_rows_kron_soft_kernel(tc, x, a, b, th, out):
             nc.sync.dma_start(out=th_pos[64 * m : 64 * m + 64, :], in_=th.rearrange("(h e) o -> h (e o)", e=2))
 
         nc.gpsimd.memset(x_raw[2][:R, :], 0.0)
-        nc.scalar.copy(out=x_raw[3][:R, :FILL], in_=x_raw[2][:R, :FILL])
-        nc.vector.memset(x_raw[3][:R, FILL:].bitcast(I32), 0)
-        for i in range(2):
+        nc.scalar.copy(out=ab_raw[:R, :FILL], in_=x_raw[2][:R, :FILL])
+        for i in (3, 0, 1):
             nc.vector.memset(x_raw[i][:R, :].bitcast(I32), 0)
-        nc.vector.memset(ab_raw[:R, :].bitcast(I32), 0)
+        nc.vector.memset(ab_raw[:R, FILL:].bitcast(I32), 0)
 
         def codes(mx, rows):
             return mx[rows, :P].bitcast(FP8X4)
@@ -94,15 +93,19 @@ def tile_rows_kron_soft_kernel(tc, x, a, b, th, out):
         nc.vector.tensor_copy(out=dst, in_=src)
         nc.vector.quantize_mx(out=codes(ab_mx, top), scales=scales(ab_mx, top), in_=ab_bf[top, :])
 
-        for i in range(1, 4):
+        for i in range(1, 3):
             dst, src = x_views(i, 0)
             nc.vector.tensor_copy(out=dst, in_=src)
-        for i in range(3):
+        for i in range(2):
             dst, src = x_views(i, 1)
             nc.scalar.copy(out=dst, in_=src)
-        dst, src = x_views(3, 1)
+        dst, src = x_views(3, 0)
         nc.scalar.copy(out=dst[:, :LAST_SCALAR], in_=src[:, :LAST_SCALAR])
         nc.vector.tensor_copy(out=dst[:, LAST_SCALAR:], in_=src[:, LAST_SCALAR:])
+        dst, src = x_views(3, 1)
+        nc.vector.tensor_copy(out=dst, in_=src)
+        dst, src = x_views(2, 1)
+        nc.scalar.copy(out=dst, in_=src)
 
         b_dst = b_bf[:].rearrange("p (c i s) -> p c s i", i=4, s=T)
         b_src = b_raw[:].rearrange("p (s c i) -> p c s i", s=T, i=4)
@@ -174,8 +177,13 @@ def tile_rows_kron_soft_kernel(tc, x, a, b, th, out):
                 nc.scalar.activation(out=up[r, e][:], in_=w_of(r, e), func=ACT.Relu, bias=bias, scale=1.0)
                 nc.scalar.activation(out=down[r, e][:], in_=w_of(r, e), func=ACT.Relu, bias=bias, scale=-1.0)
         def upper(r, e):
-            nc.vector.tensor_tensor(
-                out=up[r, e][:], in0=w_of(r, e), in1=th_pos[:, e : e + 1].to_broadcast([P, L]), op=ALU.max
+            nc.vector.tensor_scalar(
+                out=up[r, e][:],
+                in0=w_of(r, e),
+                scalar1=-1.0,
+                scalar2=th_neg[:, e : e + 1],
+                op0=ALU.mult,
+                op1=ALU.min,
             )
 
         def finish(r, e):
@@ -185,7 +193,7 @@ def tile_rows_kron_soft_kernel(tc, x, a, b, th, out):
                 scalar=th_neg[:, e : e + 1],
                 in1=up[r, e][:],
                 op0=ALU.min,
-                op1=ALU.add,
+                op1=ALU.subtract,
             )
 
         def subtract(engine, r, e):

@@ -22,6 +22,7 @@ AB_SCALAR = 10
 LAST_SCALAR = 16
 B_SCALAR = 16
 FILL = 32
+HALF = 64
 
 
 def tile_rows_kron_soft_kernel(tc, x, a, b, th, out):
@@ -61,10 +62,10 @@ def tile_rows_kron_soft_kernel(tc, x, a, b, th, out):
             nc.sync.dma_start(
                 out=x_raw[i][R:TOP, :], in_=x[2 * i : 2 * i + 2].rearrange("g (q s) j -> (g q) (s j)", s=T)
             )
-        for r in (0, 2, 1, 3):
-            nc.sync.dma_start(out=b_raw[R * r : R * r + R, :], in_=b.rearrange("(q s) c -> q (s c)", s=T))
         for m in range(2):
             nc.sync.dma_start(out=th_pos[64 * m : 64 * m + 64, :], in_=th.rearrange("(h e) o -> h (e o)", e=2))
+        for r in (0, 2, 1, 3):
+            nc.sync.dma_start(out=b_raw[R * r : R * r + R, :], in_=b.rearrange("(q s) c -> q (s c)", s=T))
 
         nc.gpsimd.memset(x_raw[2][:R, :], 0.0)
         nc.scalar.copy(out=ab_raw[:R, :FILL], in_=x_raw[2][:R, :FILL])
@@ -107,6 +108,8 @@ def tile_rows_kron_soft_kernel(tc, x, a, b, th, out):
         dst, src = x_views(2, 1)
         nc.scalar.copy(out=dst, in_=src)
 
+        nc.scalar.mul(th_neg[:], th_pos[:], -1.0)
+
         b_dst = b_bf[:].rearrange("p (c i s) -> p c s i", i=4, s=T)
         b_src = b_raw[:].rearrange("p (s c i) -> p c s i", s=T, i=4)
         nc.scalar.copy(out=b_dst[:, :B_SCALAR], in_=b_src[:, :B_SCALAR])
@@ -117,7 +120,7 @@ def tile_rows_kron_soft_kernel(tc, x, a, b, th, out):
                 scales=x_scales[t][:TOP, :],
                 in_=x_bf[:TOP, T * J * t : T * J * (t + 1)],
             )
-            for m in range(2):
+            for m in (1, 0):
                 rows = slice(R * (1 + m), R * (2 + m))
                 nc.tensor.matmul_mx(
                     out=z_ps[m][:, K * t : K * t + K],
@@ -130,9 +133,13 @@ def tile_rows_kron_soft_kernel(tc, x, a, b, th, out):
                 )
 
         nc.vector.tensor_copy(out=b_dst[:, B_SCALAR:], in_=b_src[:, B_SCALAR:])
-        nc.vector.quantize_mx(out=codes(b_mx, slice(0, P)), scales=scales(b_mx, slice(0, P)), in_=b_bf[:])
-
-        nc.scalar.mul(th_neg[:], th_pos[:], -1.0)
+        for half in range(2):
+            cols = slice(HALF * half, HALF * half + HALF)
+            nc.vector.quantize_mx(
+                out=codes(b_mx, slice(0, P))[:, cols],
+                scales=scales(b_mx, slice(0, P))[:, cols],
+                in_=b_bf[:, T * HALF * half : T * HALF * (half + 1)],
+            )
 
         def z_views(m, e):
             dst = z_bf[e][:].rearrange("p (m h t) -> p m h t", m=2, t=T)[:, m]
@@ -145,7 +152,13 @@ def tile_rows_kron_soft_kernel(tc, x, a, b, th, out):
             dst, src = z_views(1, e)
             nc.vector.tensor_copy(out=dst, in_=src)
         for e in range(2):
-            nc.vector.quantize_mx(out=z_codes[e][:].bitcast(FP8X4), scales=z_scales[e][:], in_=z_bf[e][:])
+            for m in (1 - e, e):
+                cols = slice(HALF * m, HALF * m + HALF)
+                nc.vector.quantize_mx(
+                    out=z_codes[e][:, cols].bitcast(FP8X4),
+                    scales=z_scales[e][:, cols],
+                    in_=z_bf[e][:, T * HALF * m : T * HALF * (m + 1)],
+                )
             for r in (0, 1, 3, 2):
                 rows = slice(R * r, R * r + R)
                 nc.tensor.matmul_mx(

from contextlib import ExitStack

import concourse.mybir as mybir

G, D, J, K, L = 8, 128, 128, 128, 128
FLOPS = 2 * G * D * J * K + 2 * G * J * K * L

F32 = mybir.dt.float32
BF16 = mybir.dt.bfloat16
U32 = mybir.dt.uint32
U8 = mybir.dt.uint8
I32 = mybir.dt.int32
FP8X4 = mybir.dt.float8_e4m3fn_x4
ALU = mybir.AluOpType
ACT = mybir.ActivationFunctionType

P = 128
R = 32
T = 4
TOP = 3 * R
AB_SCALAR = 10
LAST_SCALAR = 16
B_SCALAR = 16
FILL = 32
HALF = 64


def tile_rows_kron_soft_kernel(tc, x, a, b, th, out):
    nc = tc.nc
    with ExitStack() as ctx:
        sb = ctx.enter_context(tc.tile_pool(name="sb", bufs=1))
        ps = ctx.enter_context(tc.psum_pool(name="ps", bufs=1))
        ctx.enter_context(tc.manual_schedule())

        x_raw = [sb.tile([P, T * J], F32, name="x_raw%d" % i) for i in range(4)]
        ab_raw = sb.tile([P, T * K], F32)
        b_raw = sb.tile([P, T * L], F32)
        b_bf = sb.tile([P, T * L], BF16, align_bytes=64)
        th_pos = sb.tile([P, 2], F32)
        th_neg = sb.tile([P, 2], F32)
        x_bf = sb.tile([P, T * T * J], BF16, align_bytes=64)
        ab_bf = sb.tile([P, T * K], BF16, align_bytes=64)
        x_codes = [sb.tile([P, J], U32, align_bytes=64, name="x_codes%d" % t) for t in range(T)]
        x_scales = [sb.tile([P, J], U8, align_bytes=64, name="x_scales%d" % t) for t in range(T)]
        ab_mx = sb.tile([P, K + K // 4], U32, align_bytes=64)
        b_mx = sb.tile([P, L + L // 4], U32, align_bytes=64)
        z_bf = [sb.tile([P, T * K], BF16, align_bytes=64, name="z_bf%d" % m) for m in range(2)]
        z_codes = [sb.tile([P, K], U32, align_bytes=64, name="z_codes%d" % m) for m in range(2)]
        z_scales = [sb.tile([P, K], U8, align_bytes=64, name="z_scales%d" % m) for m in range(2)]
        z_ps = [ps.tile([P, T * K], F32, name="z_ps%d" % m) for m in range(2)]
        w_ps = {}
        for m in range(2):
            for r in range(4):
                if m == 1 and r in (1, 2):
                    w_ps[r, m] = z_ps[r - 1]
                else:
                    w_ps[r, m] = ps.tile([P, L], F32, name="w_ps%d_%d" % (r, m))

        for r in (1, 2):
            nc.sync.dma_start(out=ab_raw[R * r : R * r + R, :], in_=a.rearrange("(q s) c -> q (s c)", s=T))
        for i in range(4):
            nc.sync.dma_start(
                out=x_raw[i][R:TOP, :], in_=x[2 * i : 2 * i + 2].rearrange("g (q s) j -> (g q) (s j)", s=T)
            )
        for m in range(2):
            nc.sync.dma_start(out=th_pos[64 * m : 64 * m + 64, :], in_=th.rearrange("(h e) o -> h (e o)", e=2))
        for r in (0, 2, 1, 3):
            nc.sync.dma_start(out=b_raw[R * r : R * r + R, :], in_=b.rearrange("(q s) c -> q (s c)", s=T))

        nc.gpsimd.memset(x_raw[2][:R, :], 0.0)
        nc.scalar.copy(out=ab_raw[:R, :FILL], in_=x_raw[2][:R, :FILL])
        for i in (3, 0, 1):
            nc.vector.memset(x_raw[i][:R, :].bitcast(I32), 0)
        nc.vector.memset(ab_raw[:R, FILL:].bitcast(I32), 0)

        def codes(mx, rows):
            return mx[rows, :P].bitcast(FP8X4)

        def scales(mx, rows):
            return mx[rows, P:].bitcast(U8)

        def x_views(i, pair):
            ts = slice(2 * pair, 2 * pair + 2)
            dst = x_bf[:TOP, :].rearrange("p (t i u s) -> p i u s t", t=T, i=4, s=T)[:, i, :, :, ts]
            src = x_raw[i][:TOP, :].rearrange("p (s u t) -> p u s t", s=T, t=T)[:, :, :, ts]
            return dst, src

        top = slice(0, TOP)
        dst = ab_bf[top, :].rearrange("p (c i s) -> p c s i", i=4, s=T)
        src = ab_raw[top, :].rearrange("p (s c i) -> p c s i", s=T, i=4)
        nc.scalar.copy(out=dst[:, :AB_SCALAR], in_=src[:, :AB_SCALAR])
        nc.vector.tensor_copy(out=dst[:, AB_SCALAR:], in_=src[:, AB_SCALAR:])
        dst, src = x_views(0, 0)
        nc.vector.tensor_copy(out=dst, in_=src)
        nc.vector.quantize_mx(out=codes(ab_mx, top), scales=scales(ab_mx, top), in_=ab_bf[top, :])

        for i in range(1, 3):
            dst, src = x_views(i, 0)
            nc.vector.tensor_copy(out=dst, in_=src)
        for i in range(2):
            dst, src = x_views(i, 1)
            nc.scalar.copy(out=dst, in_=src)
        dst, src = x_views(3, 0)
        nc.scalar.copy(out=dst[:, :LAST_SCALAR], in_=src[:, :LAST_SCALAR])
        nc.vector.tensor_copy(out=dst[:, LAST_SCALAR:], in_=src[:, LAST_SCALAR:])
        dst, src = x_views(3, 1)
        nc.vector.tensor_copy(out=dst, in_=src)
        dst, src = x_views(2, 1)
        nc.scalar.copy(out=dst, in_=src)

        nc.scalar.mul(th_neg[:], th_pos[:], -1.0)

        b_dst = b_bf[:].rearrange("p (c i s) -> p c s i", i=4, s=T)
        b_src = b_raw[:].rearrange("p (s c i) -> p c s i", s=T, i=4)
        nc.scalar.copy(out=b_dst[:, :B_SCALAR], in_=b_src[:, :B_SCALAR])

        for t in range(T):
            nc.vector.quantize_mx(
                out=x_codes[t][:TOP, :].bitcast(FP8X4),
                scales=x_scales[t][:TOP, :],
                in_=x_bf[:TOP, T * J * t : T * J * (t + 1)],
            )
            for m in (1, 0):
                rows = slice(R * (1 + m), R * (2 + m))
                nc.tensor.matmul_mx(
                    out=z_ps[m][:, K * t : K * t + K],
                    lhsT=x_codes[t][rows, :].bitcast(FP8X4),
                    lhsT_scale=x_scales[t][rows, :],
                    rhs=codes(ab_mx, rows),
                    rhs_scale=scales(ab_mx, rows),
                    start=True,
                    stop=True,
                )

        nc.vector.tensor_copy(out=b_dst[:, B_SCALAR:], in_=b_src[:, B_SCALAR:])
        for half in range(2):
            cols = slice(HALF * half, HALF * half + HALF)
            nc.vector.quantize_mx(
                out=codes(b_mx, slice(0, P))[:, cols],
                scales=scales(b_mx, slice(0, P))[:, cols],
                in_=b_bf[:, T * HALF * half : T * HALF * (half + 1)],
            )

        def z_views(m, e):
            dst = z_bf[e][:].rearrange("p (m h t) -> p m h t", m=2, t=T)[:, m]
            src = z_ps[m][:].rearrange("p (t h e) -> p e h t", t=T, e=2)[:, e]
            return dst, src

        for e in range(2):
            dst, src = z_views(0, e)
            nc.scalar.copy(out=dst, in_=src)
            dst, src = z_views(1, e)
            nc.vector.tensor_copy(out=dst, in_=src)
        for e in range(2):
            for m in (1 - e, e):
                cols = slice(HALF * m, HALF * m + HALF)
                nc.vector.quantize_mx(
                    out=z_codes[e][:, cols].bitcast(FP8X4),
                    scales=z_scales[e][:, cols],
                    in_=z_bf[e][:, T * HALF * m : T * HALF * (m + 1)],
                )
            for r in (0, 1, 3, 2):
                rows = slice(R * r, R * r + R)
                nc.tensor.matmul_mx(
                    out=w_ps[r, e][:, :L],
                    lhsT=z_codes[e][rows, :].bitcast(FP8X4),
                    lhsT_scale=z_scales[e][rows, :],
                    rhs=codes(b_mx, rows),
                    rhs_scale=scales(b_mx, rows),
                    start=True,
                    stop=True,
                )

        y = [sb.tile([P, 2, L], F32, name="y%d" % r) for r in range(4)]
        up = {(r, e): sb.tile([P, L], F32, name="up%d_%d" % (r, e)) for r in range(4) for e in range(2)}
        down = {(r, e): sb.tile([P, L], F32, name="down%d_%d" % (r, e)) for r in (0, 3) for e in range(2)}

        def w_of(r, e):
            return w_ps[r, e][:, :L]

        def store(r):
            nc.sync.dma_start(
                out=out[2 * r : 2 * r + 2].rearrange("m (h e) l -> (m h) (e l)", e=2),
                in_=y[r][:].rearrange("p e l -> p (e l)"),
            )

        for r in (0, 3):
            for e in range(2):
                bias = th_neg[:, e : e + 1]
                nc.scalar.activation(out=up[r, e][:], in_=w_of(r, e), func=ACT.Relu, bias=bias, scale=1.0)
                nc.scalar.activation(out=down[r, e][:], in_=w_of(r, e), func=ACT.Relu, bias=bias, scale=-1.0)
        def upper(r, e):
            nc.vector.tensor_scalar(
                out=up[r, e][:],
                in0=w_of(r, e),
                scalar1=-1.0,
                scalar2=th_neg[:, e : e + 1],
                op0=ALU.mult,
                op1=ALU.min,
            )

        def finish(r, e):
            nc.vector.scalar_tensor_tensor(
                out=y[r][:, e, :],
                in0=w_of(r, e),
                scalar=th_neg[:, e : e + 1],
                in1=up[r, e][:],
                op0=ALU.min,
                op1=ALU.subtract,
            )

        def subtract(engine, r, e):
            engine.tensor_tensor(out=y[r][:, e, :], in0=up[r, e][:], in1=down[r, e][:], op=ALU.subtract)

        subtract(nc.gpsimd, 0, 0)
        subtract(nc.gpsimd, 3, 0)
        upper(1, 0)
        upper(1, 1)
        upper(2, 0)
        finish(1, 0)
        finish(1, 1)
        upper(2, 1)
        subtract(nc.vector, 0, 1)
        finish(2, 0)
        finish(2, 1)
        subtract(nc.vector, 3, 1)
        for r in (1, 0, 2, 3):
            store(r)
